import numpy as np
import ml_dtypes


def mxq(x, axis, fmt="e4m3"):
    dtype, down = {"e4m3": (ml_dtypes.float8_e4m3fn, 7), "e5m2": (ml_dtypes.float8_e5m2, 14)}[fmt]
    v = np.moveaxis(np.asarray(x, np.float32).astype(ml_dtypes.bfloat16).astype(np.float64), axis, -1)
    blocks = v.reshape(v.shape[:-1] + (-1, 32))
    amax = np.abs(blocks).max(-1, keepdims=True)
    byte = np.maximum(np.where(amax > 0, np.frexp(amax)[1] - 1 + 127, 0) - down, 1)
    scale = np.exp2(byte - 127.0)
    codes = (blocks / scale).astype(np.float32).astype(dtype).astype(np.float64)
    return np.moveaxis((codes * scale).reshape(v.shape), -1, axis)


WIDE = False


def mx_kscale(k, group=512):
    if not WIDE:
        return np.ones(k)
    levels = np.array([10, -10, 5, -5, 0])
    if group != 512:
        return np.exp2(np.random.permutation(np.resize(levels, k // group))).repeat(group)
    if k % 512:
        return np.exp2(np.random.permutation(np.resize(levels, k // 32))).repeat(32)
    a = np.empty((k // 512, 16))
    for p in range(k // 512):
        a[p, :8] = np.random.permutation(np.resize(levels, 8))
        for g in range(8):
            far = levels[np.abs(levels - a[p, g]) >= 10]
            a[p, g + 8] = far[np.random.randint(len(far))]
    return np.exp2(a.ravel()).repeat(32)


def f64(x):
    return np.asarray(x).astype(np.float64)


G, D, M, O, N = 2, 256, 128, 256, 512


def setup_inputs():
    n = np.random.standard_normal
    s_d = mx_kscale(D, 0)
    s_o = mx_kscale(O, 0)
    return {
        "x": (n((G, D, N)) * s_d[:, None]).astype(np.float32),
        "w1": (n((G, D, M)) / np.sqrt(D) / s_d[:, None]).astype(np.float32),
        "w2": (n((G, D, M)) / np.sqrt(D) / s_d[:, None]).astype(np.float32),
        "w3": (n((G, D, M)) / np.sqrt(D) / s_d[:, None]).astype(np.float32),
        "re": (np.random.uniform(0.3, 1.5, (G, M, 1))).astype(np.float32),
        "wo": (n((G, O, M)) / np.sqrt(O) / s_o[:, None]).astype(np.float32),
        "dy": (n((G, O, N)) * s_o[:, None]).astype(np.float32),
        "dx": (n((G, D, N)) * s_d[:, None]).astype(np.float32),
        "og": (np.random.uniform(0.5, 2.0, (G, M, 1))).astype(np.float32),
        "base": (0.3 * n((G, M, N))).astype(np.float32),
    }


def reference(x, w1, w2, w3, re, wo, dy, dx, og, base):
    w1q = mxq(f64(w1), 1, "e4m3")
    xq = mxq(f64(x), 1, "e4m3")
    z1 = w1q.transpose(0, 2, 1) @ xq
    dxq = mxq(f64(dx), 1, "e4m3")
    tz1 = w1q.transpose(0, 2, 1) @ dxq
    w2q = mxq(f64(w2), 1, "e4m3")
    z2 = w2q.transpose(0, 2, 1) @ xq
    tz2 = w2q.transpose(0, 2, 1) @ dxq
    w3q = mxq(f64(w3), 1, "e4m3")
    z3 = w3q.transpose(0, 2, 1) @ xq
    tz3 = w3q.transpose(0, 2, 1) @ dxq
    e1 = np.exp(z1)
    e2 = np.exp(z2)
    woq = mxq(f64(wo), 1, "e4m3")
    dyq = mxq(f64(dy), 1, "e4m3")
    c0 = woq.transpose(0, 2, 1) @ dyq
    de1 = c0 * z3 / (e1 + e2 + f64(re)) - c0 * z3 * e1 / np.square(e1 + e2 + f64(re))
    xe1 = tz1 * e1
    xe2 = tz2 * e2
    xde1 = (tz3 * c0 - (xe1 + xe2) * c0 * z3 / (e1 + e2 + f64(re))) / (e1 + e2 + f64(re)) - (tz3 * c0 * e1 + xe1 * c0 * z3 - (xe1 + xe2) * (e1 + e2 + f64(re)) * 2.0 * c0 * z3 * e1 / np.square(e1 + e2 + f64(re))) / np.square(e1 + e2 + f64(re))
    xdz1 = xde1 * e1 + xe1 * de1
    y = xdz1 * f64(og) + f64(base)
    return y

@@ -1,0 +1,204 @@
+from contextlib import ExitStack
+
+import concourse.mybir as mybir
+
+G, D, M, N = 2, 256, 128, 512
+FLOPS = 7 * 2 * G * D * M * N
+
+F32 = mybir.dt.float32
+BF16 = mybir.dt.bfloat16
+U32 = mybir.dt.uint32
+U8 = mybir.dt.uint8
+FP8X4 = mybir.dt.float8_e4m3fn_x4
+ACT = mybir.ActivationFunctionType
+ALU = mybir.AluOpType
+
+P = 128
+PACK = 4
+ROWS = D // PACK
+RUN = 4
+
+
+def tile_rows_hvtwoshare_kernel(tc, x, w1, w2, w3, re, wo, dy, dx, og, base, out):
+    nc = tc.nc
+    groups = range(G)
+
+    with ExitStack() as ctx:
+        sb = ctx.enter_context(tc.tile_pool(name="sb", bufs=1))
+        ps = ctx.enter_context(tc.psum_pool(name="ps", bufs=1))
+        ctx.enter_context(tc.manual_schedule())
+
+        def operand(name, width):
+            raw = sb.tile([P, PACK, width], F32, name=name + "_raw", align_bytes=64)
+            rounded = sb.tile([P, width, PACK], BF16, name=name + "_bf16", align_bytes=64)
+            codes = sb.tile([P, width], U32, name=name + "_codes", align_bytes=64)
+            scales = sb.tile([P, width], U8, name=name + "_scales", align_bytes=64)
+            return {"raw": raw, "rounded": rounded, "codes": codes, "scales": scales, "width": width}
+
+        def load(op, src):
+            nc.sync.dma_start(out=op["raw"][:], in_=src.rearrange("g (p j) n -> (g p) j n", j=PACK))
+
+        def views(op, lo, hi):
+            dst = op["rounded"][:, lo:hi, :].rearrange("p (c i) j -> p c j i", i=RUN)
+            src = op["raw"][:, :, lo:hi].rearrange("p j (c i) -> p c j i", i=RUN)
+            return dst, src
+
+        def round_on_vector(op, lo, hi):
+            dst, src = views(op, lo, hi)
+            nc.vector.tensor_copy(out=dst, in_=src)
+
+        def round_on_scalar(op, lo, hi):
+            dst, src = views(op, lo, hi)
+            nc.scalar.copy(out=dst, in_=src)
+
+        def round_on_gpsimd(op, lo, hi):
+            dst, src = views(op, lo, hi)
+            nc.gpsimd.tensor_scalar(out=dst, in0=src, scalar1=1.0, scalar2=0.0, op0=ALU.mult, op1=ALU.add)
+
+        def quantise(op):
+            nc.vector.quantize_mx(
+                out=op["codes"][:].bitcast(FP8X4),
+                scales=op["scales"][:],
+                in_=op["rounded"][:].rearrange("p n j -> p (n j)"),
+            )
+
+        def product(banks, weights, moving):
+            for g in groups:
+                rows = slice(g * ROWS, (g + 1) * ROWS)
+                nc.tensor.matmul_mx(
+                    out=banks[g][:],
+                    lhsT=weights["codes"][rows, :].bitcast(FP8X4),
+                    lhsT_scale=weights["scales"][rows, :],
+                    rhs=moving["codes"][rows, :].bitcast(FP8X4),
+                    rhs_scale=moving["scales"][rows, :],
+                    start=True,
+                    stop=True,
+                )
+
+        def planes(name):
+            return [sb.tile([P, N], F32, name="%s%d" % (name, g), align_bytes=64) for g in groups]
+
+        def bank(name):
+            return [ps.tile([P, N], F32, name="%s%d" % (name, g)) for g in groups]
+
+        qx, qdx, qdy = operand("x", N), operand("dx", N), operand("dy", N)
+        q1, q2, q3, qo = operand("w1", M), operand("w2", M), operand("w3", M), operand("wo", M)
+        reserve = sb.tile([P, G, 1], F32, name="reserve")
+        gain = sb.tile([P, G, 1], F32, name="gain")
+        log_reserve = sb.tile([P, G, 1], F32, name="log_reserve")
+        base_sb = sb.tile([P, G, N], F32, name="base_sb", align_bytes=64)
+        bank_a, bank_b, bank_c, bank_d = bank("bank_a"), bank("bank_b"), bank("bank_c"), bank("bank_d")
+        rest, log_rest, logit, h, w = planes("rest"), planes("log_rest"), planes("logit"), planes("h"), planes("w")
+        a, b, bz, t, e, f, ef, res = (planes(n) for n in ("a", "b", "bz", "t", "e", "f", "ef", "res"))
+        z2, tz1 = bank_a, bank_a
+        z1, c0 = bank_b, bank_b
+        tz2, tz3 = bank_c, bank_c
+        z3 = bank_d
+
+        def load_column(eng, dst, src):
+            with nc.allow_non_contiguous_dma(reason="one value a partition and group"):
+                eng.dma_start(out=dst[:], in_=src.rearrange("g m o -> m g o"))
+
+        def s_rest(g):
+            nc.scalar.activation(out=rest[g][:], in_=z2[g][:], func=ACT.Sigmoid, scale=-1.0, bias=log_reserve[:, g, :])
+
+        def s_log(g):
+            nc.scalar.activation(out=log_rest[g][:], in_=rest[g][:], func=ACT.Ln)
+
+        def s_h(g):
+            nc.scalar.activation(out=h[g][:], in_=logit[g][:], func=ACT.Tanh, scale=0.5)
+
+        def s_w(g):
+            nc.scalar.activation(out=w[g][:], in_=h[g][:], func=ACT.Square, scale=0.5)
+
+        def stt(dst, in0, scalar, in1, op0, op1):
+            nc.vector.scalar_tensor_tensor(out=dst, in0=in0, scalar=scalar, in1=in1, op0=op0, op1=op1)
+
+        def v_logit(g):
+            stt(logit[g][:], z1[g][:], log_reserve[:, g, :], log_rest[g][:], ALU.subtract, ALU.add)
+
+        def v_a(g):
+            stt(a[g][:], rest[g][:], 1.0, tz2[g][:], ALU.subtract, ALU.mult)
+
+        def v_b(g):
+            nc.vector.tensor_tensor(out=b[g][:], in0=tz1[g][:], in1=a[g][:], op=ALU.add)
+
+        def v_bz(g):
+            stt(bz[g][:], z3[g][:], gain[:, g, :], b[g][:], ALU.mult, ALU.mult)
+
+        def v_t(g, eng, lo, hi):
+            eng.tensor_tensor(out=t[g][:, lo:hi], in0=bz[g][:, lo:hi], in1=h[g][:, lo:hi], op=ALU.mult)
+
+        def v_e(g):
+            stt(e[g][:], tz3[g][:], gain[:, g, :], t[g][:], ALU.mult, ALU.subtract)
+
+        def v_f(g):
+            stt(f[g][:], w[g][:], 0.25, c0[g][:], ALU.subtract, ALU.mult)
+
+        def v_ef(g, eng, lo, hi):
+            eng.tensor_tensor(out=ef[g][:, lo:hi], in0=e[g][:, lo:hi], in1=f[g][:, lo:hi], op=ALU.mult)
+
+        def v_res(g, eng, lo, hi):
+            eng.tensor_tensor(out=res[g][:, lo:hi], in0=base_sb[:, g, lo:hi], in1=ef[g][:, lo:hi], op=ALU.subtract)
+
+        def store(g, eng, lo, hi):
+            eng.dma_start(out=out[g, :, lo:hi], in_=res[g][:, lo:hi])
+
+        def both(step):
+            for g in groups:
+                step(g)
+
+
+        load_column(nc.scalar, reserve, re)
+        load(q2, w2)
+        load(qx, x)
+        load(qdx, dx)
+        load(q1, w1)
+        load(q3, w3)
+        load(qdy, dy)
+        load(qo, wo)
+        load_column(nc.sync, gain, og)
+        nc.sync.dma_start(out=base_sb[:], in_=base.rearrange("g m n -> m g n"))
+        nc.scalar.activation(out=log_reserve[:], in_=reserve[:], func=ACT.Ln)
+        warm = sb.tile([P, G, 1], F32, name="warm")
+        nc.scalar.activation(out=warm[:], in_=reserve[:], func=ACT.Sigmoid)
+        round_on_vector(q2, 0, M)
+        quantise(q2)
+        round_on_vector(qx, 0, 352)
+        round_on_scalar(qx, 352, N)
+        quantise(qx)
+        product(z2, q2, qx)
+        both(s_rest)
+        round_on_vector(qdx, 0, N)
+        round_on_vector(q1, 0, M)
+        quantise(qdx)
+        quantise(q1)
+        product(tz2, q2, qdx)
+        product(z1, q1, qx)
+        product(tz1, q1, qdx)
+        both(s_log)
+        round_on_vector(q3, 0, M)
+        both(v_a)
+        quantise(q3)
+        product(z3, q3, qx)
+        product(tz3, q3, qdx)
+        both(v_b)
+        round_on_scalar(qdy, 0, N)
+        both(v_logit)
+        both(s_h)
+        both(s_w)
+        round_on_vector(qo, 0, M)
+        both(v_bz)
+        quantise(qo)
+        quantise(qdy)
+        product(c0, qo, qdy)
+        v_t(0, nc.vector, 0, N)
+        v_t(1, nc.vector, 0, N)
+        both(v_e)
+        both(v_f)
+        v_ef(0, nc.vector, 0, N)
+        v_ef(1, nc.vector, 0, N)
+        v_res(0, nc.vector, 0, N)
+        store(0, nc.sync, 0, N)
+        v_res(1, nc.vector, 0, N)
+        store(1, nc.scalar, 0, N)

@@ -52,7 +52,8 @@ def tile_rows_hvtwoshare_kernel(tc, x, w1, w2, w3, re, wo, dy, dx, og, base, out
             nc.scalar.copy(out=dst, in_=src)
 
         def round_on_gpsimd(op, lo, hi):
-            dst, src = views(op, lo, hi)
+            dst = op["rounded"][:, lo:hi, :]
+            src = op["raw"][:, :, lo:hi].rearrange("p j n -> p n j")
             nc.gpsimd.tensor_scalar(out=dst, in0=src, scalar1=1.0, scalar2=0.0, op0=ALU.mult, op1=ALU.add)
 
         def quantise(op):
@@ -149,9 +150,9 @@ def tile_rows_hvtwoshare_kernel(tc, x, w1, w2, w3, re, wo, dy, dx, og, base, out
                 step(g)
 
 
-        load_column(nc.scalar, reserve, re)
-        load(q2, w2)
+        load_column(nc.sync, reserve, re)
         load(qx, x)
+        load(q2, w2)
         load(qdx, dx)
         load(q1, w1)
         load(q3, w3)
@@ -162,40 +163,42 @@ def tile_rows_hvtwoshare_kernel(tc, x, w1, w2, w3, re, wo, dy, dx, og, base, out
         nc.scalar.activation(out=log_reserve[:], in_=reserve[:], func=ACT.Ln)
         warm = sb.tile([P, G, 1], F32, name="warm")
         nc.scalar.activation(out=warm[:], in_=reserve[:], func=ACT.Sigmoid)
-        round_on_vector(q2, 0, M)
-        quantise(q2)
         round_on_vector(qx, 0, 352)
         round_on_scalar(qx, 352, N)
+        round_on_scalar(q2, 0, M)
         quantise(qx)
+        quantise(q2)
         product(z2, q2, qx)
         both(s_rest)
         round_on_vector(qdx, 0, N)
         round_on_vector(q1, 0, M)
         quantise(qdx)
+        round_on_vector(q3, 0, M)
         quantise(q1)
+        quantise(q3)
         product(tz2, q2, qdx)
         product(z1, q1, qx)
         product(tz1, q1, qdx)
-        both(s_log)
-        round_on_vector(q3, 0, M)
-        both(v_a)
-        quantise(q3)
         product(z3, q3, qx)
+        both(s_log)
+        both(v_a)
         product(tz3, q3, qdx)
-        both(v_b)
-        round_on_scalar(qdy, 0, N)
+        round_on_gpsimd(qdy, 0, 192)
+        round_on_gpsimd(qdy, 192, 384)
+        round_on_scalar(qdy, 384, N)
+        round_on_scalar(qo, 0, M)
         both(v_logit)
         both(s_h)
         both(s_w)
-        round_on_vector(qo, 0, M)
-        both(v_bz)
-        quantise(qo)
+        both(v_b)
         quantise(qdy)
+        quantise(qo)
         product(c0, qo, qdy)
-        v_t(0, nc.vector, 0, N)
-        v_t(1, nc.vector, 0, N)
-        both(v_e)
+        both(v_bz)
+        v_t(0, nc.gpsimd, 0, N)
+        v_t(1, nc.gpsimd, 0, N)
         both(v_f)
+        both(v_e)
         v_ef(0, nc.vector, 0, N)
         v_ef(1, nc.vector, 0, N)
         v_res(0, nc.vector, 0, N)

@@ -161,8 +161,6 @@ def tile_rows_hvtwoshare_kernel(tc, x, w1, w2, w3, re, wo, dy, dx, og, base, out
         load_column(nc.sync, gain, og)
         nc.sync.dma_start(out=base_sb[:], in_=base.rearrange("g m n -> m g n"))
         nc.scalar.activation(out=log_reserve[:], in_=reserve[:], func=ACT.Ln)
-        warm = sb.tile([P, G, 1], F32, name="warm")
-        nc.scalar.activation(out=warm[:], in_=reserve[:], func=ACT.Sigmoid)
         round_on_vector(qx, 0, 352)
         round_on_scalar(qx, 352, N)
         round_on_scalar(q2, 0, M)

from contextlib import ExitStack

import concourse.mybir as mybir

G, D, M, N = 2, 256, 128, 512
FLOPS = 7 * 2 * G * D * M * N

F32 = mybir.dt.float32
BF16 = mybir.dt.bfloat16
U32 = mybir.dt.uint32
U8 = mybir.dt.uint8
FP8X4 = mybir.dt.float8_e4m3fn_x4
ACT = mybir.ActivationFunctionType
ALU = mybir.AluOpType

P = 128
PACK = 4
ROWS = D // PACK
RUN = 4


def tile_rows_hvtwoshare_kernel(tc, x, w1, w2, w3, re, wo, dy, dx, og, base, out):
    nc = tc.nc
    groups = range(G)

    with ExitStack() as ctx:
        sb = ctx.enter_context(tc.tile_pool(name="sb", bufs=1))
        ps = ctx.enter_context(tc.psum_pool(name="ps", bufs=1))
        ctx.enter_context(tc.manual_schedule())

        def operand(name, width):
            raw = sb.tile([P, PACK, width], F32, name=name + "_raw", align_bytes=64)
            rounded = sb.tile([P, width, PACK], BF16, name=name + "_bf16", align_bytes=64)
            codes = sb.tile([P, width], U32, name=name + "_codes", align_bytes=64)
            scales = sb.tile([P, width], U8, name=name + "_scales", align_bytes=64)
            return {"raw": raw, "rounded": rounded, "codes": codes, "scales": scales, "width": width}

        def load(op, src):
            nc.sync.dma_start(out=op["raw"][:], in_=src.rearrange("g (p j) n -> (g p) j n", j=PACK))

        def views(op, lo, hi):
            dst = op["rounded"][:, lo:hi, :].rearrange("p (c i) j -> p c j i", i=RUN)
            src = op["raw"][:, :, lo:hi].rearrange("p j (c i) -> p c j i", i=RUN)
            return dst, src

        def round_on_vector(op, lo, hi):
            dst, src = views(op, lo, hi)
            nc.vector.tensor_copy(out=dst, in_=src)

        def round_on_scalar(op, lo, hi):
            dst, src = views(op, lo, hi)
            nc.scalar.copy(out=dst, in_=src)

        def round_on_gpsimd(op, lo, hi):
            dst = op["rounded"][:, lo:hi, :]
            src = op["raw"][:, :, lo:hi].rearrange("p j n -> p n j")
            nc.gpsimd.tensor_scalar(out=dst, in0=src, scalar1=1.0, scalar2=0.0, op0=ALU.mult, op1=ALU.add)

        def quantise(op):
            nc.vector.quantize_mx(
                out=op["codes"][:].bitcast(FP8X4),
                scales=op["scales"][:],
                in_=op["rounded"][:].rearrange("p n j -> p (n j)"),
            )

        def product(banks, weights, moving):
            for g in groups:
                rows = slice(g * ROWS, (g + 1) * ROWS)
                nc.tensor.matmul_mx(
                    out=banks[g][:],
                    lhsT=weights["codes"][rows, :].bitcast(FP8X4),
                    lhsT_scale=weights["scales"][rows, :],
                    rhs=moving["codes"][rows, :].bitcast(FP8X4),
                    rhs_scale=moving["scales"][rows, :],
                    start=True,
                    stop=True,
                )

        def planes(name):
            return [sb.tile([P, N], F32, name="%s%d" % (name, g), align_bytes=64) for g in groups]

        def bank(name):
            return [ps.tile([P, N], F32, name="%s%d" % (name, g)) for g in groups]

        qx, qdx, qdy = operand("x", N), operand("dx", N), operand("dy", N)
        q1, q2, q3, qo = operand("w1", M), operand("w2", M), operand("w3", M), operand("wo", M)
        reserve = sb.tile([P, G, 1], F32, name="reserve")
        gain = sb.tile([P, G, 1], F32, name="gain")
        log_reserve = sb.tile([P, G, 1], F32, name="log_reserve")
        base_sb = sb.tile([P, G, N], F32, name="base_sb", align_bytes=64)
        bank_a, bank_b, bank_c, bank_d = bank("bank_a"), bank("bank_b"), bank("bank_c"), bank("bank_d")
        rest, log_rest, logit, h, w = planes("rest"), planes("log_rest"), planes("logit"), planes("h"), planes("w")
        a, b, bz, t, e, f, ef, res = (planes(n) for n in ("a", "b", "bz", "t", "e", "f", "ef", "res"))
        z2, tz1 = bank_a, bank_a
        z1, c0 = bank_b, bank_b
        tz2, tz3 = bank_c, bank_c
        z3 = bank_d

        def load_column(eng, dst, src):
            with nc.allow_non_contiguous_dma(reason="one value a partition and group"):
                eng.dma_start(out=dst[:], in_=src.rearrange("g m o -> m g o"))

        def s_rest(g):
            nc.scalar.activation(out=rest[g][:], in_=z2[g][:], func=ACT.Sigmoid, scale=-1.0, bias=log_reserve[:, g, :])

        def s_log(g):
            nc.scalar.activation(out=log_rest[g][:], in_=rest[g][:], func=ACT.Ln)

        def s_h(g):
            nc.scalar.activation(out=h[g][:], in_=logit[g][:], func=ACT.Tanh, scale=0.5)

        def s_w(g):
            nc.scalar.activation(out=w[g][:], in_=h[g][:], func=ACT.Square, scale=0.5)

        def stt(dst, in0, scalar, in1, op0, op1):
            nc.vector.scalar_tensor_tensor(out=dst, in0=in0, scalar=scalar, in1=in1, op0=op0, op1=op1)

        def v_logit(g):
            stt(logit[g][:], z1[g][:], log_reserve[:, g, :], log_rest[g][:], ALU.subtract, ALU.add)

        def v_a(g):
            stt(a[g][:], rest[g][:], 1.0, tz2[g][:], ALU.subtract, ALU.mult)

        def v_b(g):
            nc.vector.tensor_tensor(out=b[g][:], in0=tz1[g][:], in1=a[g][:], op=ALU.add)

        def v_bz(g):
            stt(bz[g][:], z3[g][:], gain[:, g, :], b[g][:], ALU.mult, ALU.mult)

        def v_t(g, eng, lo, hi):
            eng.tensor_tensor(out=t[g][:, lo:hi], in0=bz[g][:, lo:hi], in1=h[g][:, lo:hi], op=ALU.mult)

        def v_e(g):
            stt(e[g][:], tz3[g][:], gain[:, g, :], t[g][:], ALU.mult, ALU.subtract)

        def v_f(g):
            stt(f[g][:], w[g][:], 0.25, c0[g][:], ALU.subtract, ALU.mult)

        def v_ef(g, eng, lo, hi):
            eng.tensor_tensor(out=ef[g][:, lo:hi], in0=e[g][:, lo:hi], in1=f[g][:, lo:hi], op=ALU.mult)

        def v_res(g, eng, lo, hi):
            eng.tensor_tensor(out=res[g][:, lo:hi], in0=base_sb[:, g, lo:hi], in1=ef[g][:, lo:hi], op=ALU.subtract)

        def store(g, eng, lo, hi):
            eng.dma_start(out=out[g, :, lo:hi], in_=res[g][:, lo:hi])

        def both(step):
            for g in groups:
                step(g)


        load_column(nc.sync, reserve, re)
        load(qx, x)
        load(q2, w2)
        load(qdx, dx)
        load(q1, w1)
        load(q3, w3)
        load(qdy, dy)
        load(qo, wo)
        load_column(nc.sync, gain, og)
        nc.sync.dma_start(out=base_sb[:], in_=base.rearrange("g m n -> m g n"))
        nc.scalar.activation(out=log_reserve[:], in_=reserve[:], func=ACT.Ln)
        round_on_vector(qx, 0, 352)
        round_on_scalar(qx, 352, N)
        round_on_scalar(q2, 0, M)
        quantise(qx)
        quantise(q2)
        product(z2, q2, qx)
        both(s_rest)
        round_on_vector(qdx, 0, N)
        round_on_vector(q1, 0, M)
        quantise(qdx)
        round_on_vector(q3, 0, M)
        quantise(q1)
        quantise(q3)
        product(tz2, q2, qdx)
        product(z1, q1, qx)
        product(tz1, q1, qdx)
        product(z3, q3, qx)
        both(s_log)
        both(v_a)
        product(tz3, q3, qdx)
        round_on_gpsimd(qdy, 0, 192)
        round_on_gpsimd(qdy, 192, 384)
        round_on_scalar(qdy, 384, N)
        round_on_scalar(qo, 0, M)
        both(v_logit)
        both(s_h)
        both(s_w)
        both(v_b)
        quantise(qdy)
        quantise(qo)
        product(c0, qo, qdy)
        both(v_bz)
        v_t(0, nc.gpsimd, 0, N)
        v_t(1, nc.gpsimd, 0, N)
        both(v_f)
        both(v_e)
        v_ef(0, nc.vector, 0, N)
        v_ef(1, nc.vector, 0, N)
        v_res(0, nc.vector, 0, N)
        store(0, nc.sync, 0, N)
        v_res(1, nc.vector, 0, N)
        store(1, nc.scalar, 0, N)
